import numpy as np
import ml_dtypes


def mxq(x, axis, fmt="e4m3"):
    dtype, down = {"e4m3": (ml_dtypes.float8_e4m3fn, 7), "e5m2": (ml_dtypes.float8_e5m2, 14)}[fmt]
    v = np.moveaxis(np.asarray(x, np.float32).astype(ml_dtypes.bfloat16).astype(np.float64), axis, -1)
    blocks = v.reshape(v.shape[:-1] + (-1, 32))
    amax = np.abs(blocks).max(-1, keepdims=True)
    byte = np.maximum(np.where(amax > 0, np.frexp(amax)[1] - 1 + 127, 0) - down, 1)
    scale = np.exp2(byte - 127.0)
    codes = (blocks / scale).astype(np.float32).astype(dtype).astype(np.float64)
    return np.moveaxis((codes * scale).reshape(v.shape), -1, axis)


WIDE = False


def mx_kscale(k):
    if not WIDE:
        return np.ones(k)
    levels = np.array([10, -10, 5, -5, 0])
    if k % 512:
        return np.exp2(np.random.permutation(np.resize(levels, k // 32))).repeat(32)
    a = np.empty((k // 512, 16))
    for p in range(k // 512):
        a[p, :8] = np.random.permutation(np.resize(levels, 8))
        for g in range(8):
            far = levels[np.abs(levels - a[p, g]) >= 10]
            a[p, g + 8] = far[np.random.randint(len(far))]
    return np.exp2(a.ravel()).repeat(32)


def f64(x):
    return np.asarray(x).astype(np.float64)


def striped(idx):
    return np.tile(np.asarray(idx).reshape(-1, 16).T, (8, 1)).astype(np.uint16)


def unstriped(offs):
    return offs[:16].T.reshape(-1).astype(np.int64)


E2M1 = np.array([0.0, 0.5, 1.0, 1.5, 2.0, 3.0, 4.0, 6.0, -0.0, -0.5, -1.0, -1.5, -2.0, -3.0, -4.0, -6.0])


def pack_weight(w, fmt):
    k, n = w.shape
    w = f64(np.asarray(w, np.float32).astype(ml_dtypes.bfloat16)).reshape(k // 32, 32, n)
    amax = np.abs(w).max(1)
    if fmt == "e4m3":
        byte = np.frexp(amax)[1] - 1 + 127 - 7
    else:
        mant, ex = np.frexp(amax / 6.0)
        byte = np.where(mant > 0.5, ex, ex - 1) + 127
    byte = np.clip(np.where(amax > 0, byte, 1), 1, 254)
    scaled = (w * np.exp2(127.0 - byte)[:, None, :]).reshape(k, n).astype(np.float32)
    by_word = np.ascontiguousarray(scaled.reshape(k // 512, 128, 4, n).transpose(0, 1, 3, 2))
    if fmt == "e4m3":
        words = by_word.astype(ml_dtypes.float8_e4m3fn).view(np.uint8)
    else:
        c = by_word.astype(ml_dtypes.float4_e2m1fn).view(np.uint8) & 0xF
        words = (c[..., 0::2] | (c[..., 1::2] << 4)).reshape(k // 512, 128, 2 * n)
    return np.ascontiguousarray(words), np.ascontiguousarray(byte.astype(np.uint8).reshape(k // 512, 16, n))


def unpack_weight(words, scales, fmt):
    g, _, n = scales.shape
    words = np.ascontiguousarray(words).reshape(g, 128, n, -1)
    if fmt == "e4m3":
        vals = words.view(ml_dtypes.float8_e4m3fn).astype(np.float64)
    else:
        nib = np.empty((g, 128, n, 4), np.uint8)
        nib[..., 0::2] = words & 0xF
        nib[..., 1::2] = words >> 4
        vals = E2M1[nib]
    vals = vals * np.repeat(np.exp2(scales.astype(np.float64) - 127.0), 8, axis=1)[..., None]
    return vals.transpose(0, 1, 3, 2).reshape(g * 512, n)


def e4m3fn_bytes(y):
    return np.clip(np.asarray(y, np.float64), -448.0, 448.0).astype(np.float32).astype(ml_dtypes.float8_e4m3fn).view(np.uint8)


def e4m3fn_values(b):
    return np.asarray(b, np.uint8).view(ml_dtypes.float8_e4m3fn).astype(np.float64)


K, T, J, R, F, Z, V, D, N = 512, 1024, 256, 512, 512, 1024, 1024, 512, 256


def setup_inputs():
    n = np.random.standard_normal
    idx = np.random.permutation(T)[:J]
    idx2 = np.random.permutation(Z)[:J]
    idx3 = np.random.permutation(V)[:J]
    idx4 = np.random.permutation(D)[:J]
    fk = mx_kscale(K)
    ff = mx_kscale(F)
    fr = mx_kscale(R)
    xtp = pack_weight(n((K, T)) / fk[:, None], "e2m1")
    xop = pack_weight(n((F, Z)) / ff[:, None], "e4m3")
    wp = pack_weight(n((K, R)) * 1 / np.sqrt(K) * fk[:, None], "e4m3")
    w2p = pack_weight(n((F, R)) * 1 / np.sqrt(F) * ff[:, None] * fr, "e2m1")
    wbp = pack_weight(n((R, N)) * 1 / np.sqrt(R) / fr[:, None], "e2m1")
    return {
        "xt_words": xtp[0],
        "xt_scales": xtp[1],
        "xo_words": xop[0],
        "xo_scales": xop[1],
        "w_words": wp[0],
        "w_scales": wp[1],
        "w2_words": w2p[0],
        "w2_scales": w2p[1],
        "ca": e4m3fn_bytes(8.0 * n((R, V))),
        "cb": e4m3fn_bytes(8.0 * n((R, D))),
        "st": (np.random.uniform(0.01, 0.03, (R, 1)) * fr[:, None]).astype(np.float32),
        "wb_words": wbp[0],
        "wb_scales": wbp[1],
        "offs": striped(idx),
        "offs2": striped(idx2),
        "offs3": striped(idx3),
        "offs4": striped(idx4),
    }


def reference(xt_words, xt_scales, xo_words, xo_scales, w_words, w_scales, w2_words, w2_scales, ca, cb, st, wb_words, wb_scales, offs, offs2, offs3, offs4):
    idx = unstriped(offs)
    idx2 = unstriped(offs2)
    idx3 = unstriped(offs3)
    idx4 = unstriped(offs4)
    xtu = unpack_weight(xt_words, xt_scales, "e2m1")
    xou = unpack_weight(xo_words, xo_scales, "e4m3")
    wu = unpack_weight(w_words, w_scales, "e4m3")
    w2u = unpack_weight(w2_words, w2_scales, "e2m1")
    wbu = unpack_weight(wb_words, wb_scales, "e2m1")
    xtidxg = xtu[:, idx]
    a = wu.T @ xtidxg
    xoidx2g = xou[:, idx2]
    b = w2u.T @ xoidx2g
    g1 = e4m3fn_values(ca)[:, idx3] * e4m3fn_values(cb)[:, idx4] * f64(st)
    hid = np.maximum(a * g1, b)
    hidq = mxq(hid, 0, "e4m3")
    p = wbu.T @ hidq
    return p

@@ -1,0 +1,179 @@
+from contextlib import ExitStack
+
+import concourse.mybir as mybir
+
+F32 = mybir.dt.float32
+BF16 = mybir.dt.bfloat16
+I32 = mybir.dt.int32
+U32 = mybir.dt.uint32
+U16 = mybir.dt.uint16
+U8 = mybir.dt.uint8
+FP8 = mybir.dt.float8_e4m3fn
+FP8X4 = mybir.dt.float8_e4m3fn_x4
+FP4X4 = mybir.dt.float4_e2m1fn_x4
+MULT = mybir.AluOpType.mult
+MAX = mybir.AluOpType.max
+COPY = mybir.ActivationFunctionType.Copy
+
+P = 128
+PACK = 4
+T, J, R, Z, V, D, N = 1024, 256, 512, 1024, 1024, 512, 256
+HALF = J // 2
+FLOPS = 2 * 512 * R * J * 2 + 2 * R * N * J
+
+
+def tile_list_productentries_kernel(
+    tc, xt_words, xt_scales, xo_words, xo_scales, w_words, w_scales, w2_words, w2_scales,
+    ca, cb, st, wb_words, wb_scales, offs, offs2, offs3, offs4, out,
+):
+    nc = tc.nc
+    with ExitStack() as ctx:
+        sb = ctx.enter_context(tc.tile_pool(name="sb", bufs=1))
+        ps = ctx.enter_context(tc.psum_pool(name="ps", bufs=1))
+
+        def tile(name, shape, dtype):
+            return sb.tile(shape, dtype, name=name, align_bytes=64)
+
+        def load_list(name, src):
+            lst = tile(name, [P, J // 16], U16)
+            nc.sync.dma_start(lst[:], src)
+            return lst
+
+        def load_words(name, src, width, dtype):
+            words = tile(name, [P, width], dtype)
+            nc.sync.dma_start(words[:].bitcast(I32), src.bitcast(I32))
+            return words
+
+        def zero_plane(engine, name, width):
+            plane = tile(name, [P, width], U8)
+            engine.memset(plane[:].bitcast(I32), 0)
+            return plane
+
+        def load_plane(queue, plane, src):
+            for q in range(4):
+                queue.dma_start(
+                    plane[32 * q : 32 * q + 4, :].bitcast(I32), src[0, 4 * q : 4 * q + 4, :].bitcast(I32)
+                )
+
+        def load_table(name, rows, width):
+            table = tile(name, [P, width], U8)
+            nc.sync.dma_start(table[:], rows)
+            return table
+
+        ca_rows = ca.rearrange("(p t) v -> t p v", t=PACK)
+        cb_rows = cb.rearrange("(p t) d -> t p d", t=PACK)
+        step = tile("step", [P, PACK], F32)
+        cb_tab = {}
+        ca_tab = {}
+
+        nc.gpsimd.dma_start(step[:], st.rearrange("(p t) o -> p (t o)", t=PACK))
+        wb_plane = zero_plane(nc.gpsimd, "wb_plane", N)
+        load_plane(nc.gpsimd, wb_plane, wb_scales)
+        xt_plane = zero_plane(nc.vector, "xt_plane", T)
+        w_plane = zero_plane(nc.vector, "w_plane", R)
+        xo_plane = zero_plane(nc.vector, "xo_plane", Z)
+        w2_plane = zero_plane(nc.vector, "w2_plane", R)
+
+        list4 = load_list("list4", offs4)
+        cb_tab[0] = load_table("cb_tab0", cb_rows[0], D)
+        list3 = load_list("list3", offs3)
+        ca_tab[0] = load_table("ca_tab0", ca_rows[0], V)
+        cb_tab[1] = load_table("cb_tab1", cb_rows[1], D)
+        ca_tab[1] = load_table("ca_tab1", ca_rows[1], V)
+        list1 = load_list("list1", offs)
+        list2 = load_list("list2", offs2)
+        for t in (2, 3):
+            cb_tab[t] = load_table("cb_tab%d" % t, cb_rows[t], D)
+            ca_tab[t] = load_table("ca_tab%d" % t, ca_rows[t], V)
+        load_plane(nc.sync, xt_plane, xt_scales)
+        w = load_words("w", w_words[0].rearrange("p n t -> p (n t)"), R, U32)
+        xt = load_words("xt", xt_words[0], T, U16)
+        load_plane(nc.sync, w_plane, w_scales)
+        w2 = load_words("w2", w2_words[0], R, U16)
+        xo = load_words("xo", xo_words[0].rearrange("p n t -> p (n t)"), Z, U32)
+        load_plane(nc.sync, w2_plane, w2_scales)
+        load_plane(nc.sync, xo_plane, xo_scales)
+        wb = load_words("wb", wb_words[0], N, U16)
+
+        ca_pick = tile("ca_pick", [P, PACK, J], U8)
+        cb_pick = tile("cb_pick", [P, PACK, J], U8)
+        cb_step = tile("cb_step", [P, PACK, J], F32)
+        gate = tile("gate", [P, PACK, J], F32)
+        for t in range(PACK):
+            nc.vector.tensor_copy(cb_pick[:, t, :], cb_tab[t][:].indirect(list4[:]))
+            nc.vector.tensor_copy(ca_pick[:, t, :], ca_tab[t][:].indirect(list3[:]))
+            nc.scalar.activation(
+                out=cb_step[:, t, :], in_=cb_pick[:, t, :].bitcast(FP8), func=COPY, scale=step[:, t : t + 1]
+            )
+            nc.vector.tensor_tensor(gate[:, t, :], ca_pick[:, t, :].bitcast(FP8), cb_step[:, t, :], MULT)
+
+        gate_woven = []
+        for h in range(2):
+            woven = tile("gate_woven%d" % h, [P, HALF, PACK], F32)
+            nc.scalar.copy(woven[:], gate[:, :, h * HALF : (h + 1) * HALF].rearrange("p t j -> p j t"))
+            gate_woven.append(woven)
+
+        def first_stage(name, lst, x, x_plane, x_dt, x_mx, wt, wt_plane, wt_dt, wt_mx):
+            wt_dealt = tile(name + "_w_dealt", [P, PACK, P], wt_dt)
+            nc.scalar.copy(wt_dealt[:], wt[:].rearrange("p (m t) -> p t m", t=PACK))
+            ws_dealt = tile(name + "_ws_dealt", [P, PACK, P], U8)
+            nc.vector.tensor_copy(ws_dealt[:], wt_plane[:].rearrange("p (m t) -> p t m", t=PACK))
+            x_pick = tile(name + "_x_pick", [P, J], x_dt)
+            nc.vector.tensor_copy(x_pick[:], x[:].indirect(lst[:]))
+            xs_pick = tile(name + "_xs_pick", [P, J], U8)
+            nc.vector.tensor_copy(xs_pick[:], x_plane[:].indirect(lst[:]))
+            banks = []
+            for h in range(2):
+                bank = ps.tile([P, PACK, HALF], F32, name="%s_sum%d" % (name, h))
+                cols = slice(h * HALF, (h + 1) * HALF)
+                for t in range(PACK):
+                    nc.tensor.matmul_mx(
+                        out=bank[:, t, :],
+                        lhsT=wt_dealt[:, t, :].bitcast(wt_mx),
+                        lhsT_scale=ws_dealt[:, t, :],
+                        rhs=x_pick[:, cols].bitcast(x_mx),
+                        rhs_scale=xs_pick[:, cols],
+                        start=True,
+                        stop=True,
+                    )
+                banks.append(bank)
+            return banks
+
+        a_sum = first_stage("a", list1, xt, xt_plane, U16, FP4X4, w, w_plane, U32, FP8X4)
+        b_sum = first_stage("b", list2, xo, xo_plane, U32, FP8X4, w2, w2_plane, U16, FP4X4)
+
+        gated = []
+        for h in range(2):
+            prod = tile("gated%d" % h, [P, HALF, PACK], F32)
+            nc.vector.tensor_tensor(prod[:], a_sum[h][:].rearrange("p t j -> p j t"), gate_woven[h][:], MULT)
+            gated.append(prod)
+        hid = []
+        for h in range(2):
+            larger = tile("hid%d" % h, [P, HALF, PACK], BF16)
+            nc.vector.tensor_tensor(larger[:], b_sum[h][:].rearrange("p t j -> p j t"), gated[h][:], MAX)
+            hid.append(larger)
+
+        out_rows = out.rearrange("(c p) j -> p c j", p=P)
+        for h in range(2):
+            codes = tile("hid_codes%d" % h, [P, HALF], U32)
+            scales = tile("hid_scales%d" % h, [P, HALF], U8)
+            nc.vector.quantize_mx(
+                out=codes[:].bitcast(FP8X4), scales=scales[:], in_=hid[h][:].rearrange("p j t -> p (j t)")
+            )
+            result = tile("result%d" % h, [P, N // P, HALF], F32)
+            for c in range(N // P):
+                acc = ps.tile([P, HALF], F32, name="out_sum%d_%d" % (h, c))
+                nc.tensor.matmul_mx(
+                    out=acc[:],
+                    lhsT=wb[:, c * P : (c + 1) * P].bitcast(FP4X4),
+                    lhsT_scale=wb_plane[:, c * P : (c + 1) * P],
+                    rhs=codes[:].bitcast(FP8X4),
+                    rhs_scale=scales[:],
+                    start=True,
+                    stop=True,
+                )
+                if h == 1 and c == 1:
+                    nc.vector.tensor_copy(result[:, c, :], acc[:])
+                else:
+                    nc.scalar.copy(result[:, c, :], acc[:])
+            nc.sync.dma_start(out_rows[:, :, h * HALF : (h + 1) * HALF], result[:])

@@ -66,34 +66,31 @@ def tile_list_productentries_kernel(
         cb_tab = {}
         ca_tab = {}
 
-        nc.gpsimd.dma_start(step[:], st.rearrange("(p t) o -> p (t o)", t=PACK))
-        wb_plane = zero_plane(nc.gpsimd, "wb_plane", N)
-        load_plane(nc.gpsimd, wb_plane, wb_scales)
         xt_plane = zero_plane(nc.vector, "xt_plane", T)
         w_plane = zero_plane(nc.vector, "w_plane", R)
-        xo_plane = zero_plane(nc.vector, "xo_plane", Z)
         w2_plane = zero_plane(nc.vector, "w2_plane", R)
+        xo_plane = zero_plane(nc.vector, "xo_plane", Z)
+        wb_plane = zero_plane(nc.vector, "wb_plane", N)
 
         list4 = load_list("list4", offs4)
-        cb_tab[0] = load_table("cb_tab0", cb_rows[0], D)
-        list3 = load_list("list3", offs3)
-        ca_tab[0] = load_table("ca_tab0", ca_rows[0], V)
-        cb_tab[1] = load_table("cb_tab1", cb_rows[1], D)
-        ca_tab[1] = load_table("ca_tab1", ca_rows[1], V)
-        list1 = load_list("list1", offs)
-        list2 = load_list("list2", offs2)
-        for t in (2, 3):
+        for t in range(PACK):
             cb_tab[t] = load_table("cb_tab%d" % t, cb_rows[t], D)
+        nc.sync.dma_start(step[:], st.rearrange("(p t) o -> p (t o)", t=PACK))
+        list3 = load_list("list3", offs3)
+        for t in range(PACK):
             ca_tab[t] = load_table("ca_tab%d" % t, ca_rows[t], V)
+        list1 = load_list("list1", offs)
         load_plane(nc.sync, xt_plane, xt_scales)
-        w = load_words("w", w_words[0].rearrange("p n t -> p (n t)"), R, U32)
-        xt = load_words("xt", xt_words[0], T, U16)
         load_plane(nc.sync, w_plane, w_scales)
-        w2 = load_words("w2", w2_words[0], R, U16)
+        xt = load_words("xt", xt_words[0], T, U16)
+        list2 = load_list("list2", offs2)
         xo = load_words("xo", xo_words[0].rearrange("p n t -> p (n t)"), Z, U32)
         load_plane(nc.sync, w2_plane, w2_scales)
+        w = load_words("w", w_words[0].rearrange("p n t -> p (n t)"), R, U32)
         load_plane(nc.sync, xo_plane, xo_scales)
+        w2 = load_words("w2", w2_words[0], R, U16)
         wb = load_words("wb", wb_words[0], N, U16)
+        load_plane(nc.sync, wb_plane, wb_scales)
 
         ca_pick = tile("ca_pick", [P, PACK, J], U8)
         cb_pick = tile("cb_pick", [P, PACK, J], U8)
@@ -101,11 +98,12 @@ def tile_list_productentries_kernel(
         gate = tile("gate", [P, PACK, J], F32)
         for t in range(PACK):
             nc.vector.tensor_copy(cb_pick[:, t, :], cb_tab[t][:].indirect(list4[:]))
-            nc.vector.tensor_copy(ca_pick[:, t, :], ca_tab[t][:].indirect(list3[:]))
             nc.scalar.activation(
                 out=cb_step[:, t, :], in_=cb_pick[:, t, :].bitcast(FP8), func=COPY, scale=step[:, t : t + 1]
             )
-            nc.vector.tensor_tensor(gate[:, t, :], ca_pick[:, t, :].bitcast(FP8), cb_step[:, t, :], MULT)
+        for t in range(PACK):
+            nc.vector.tensor_copy(ca_pick[:, t, :], ca_tab[t][:].indirect(list3[:]))
+        nc.vector.tensor_tensor(gate[:], ca_pick[:].bitcast(FP8), cb_step[:], MULT)
 
         gate_woven = []
         for h in range(2):

@@ -31,8 +31,8 @@ def tile_list_productentries_kernel(
         sb = ctx.enter_context(tc.tile_pool(name="sb", bufs=1))
         ps = ctx.enter_context(tc.psum_pool(name="ps", bufs=1))
 
-        def tile(name, shape, dtype):
-            return sb.tile(shape, dtype, name=name, align_bytes=64)
+        def tile(name, shape, dtype, tag=""):
+            return sb.tile(shape, dtype, name=name, tag=tag, align_bytes=64)
 
         def load_list(name, src):
             lst = tile(name, [P, J // 16], U16)
@@ -45,7 +45,7 @@ def tile_list_productentries_kernel(
             return words
 
         def zero_plane(engine, name, width):
-            plane = tile(name, [P, width], U8)
+            plane = tile(name, [P, width], U8, tag=name)
             engine.memset(plane[:].bitcast(I32), 0)
             return plane
 
@@ -79,14 +79,14 @@ def tile_list_productentries_kernel(
         list3 = load_list("list3", offs3)
         for t in range(PACK):
             ca_tab[t] = load_table("ca_tab%d" % t, ca_rows[t], V)
+        w = load_words("w", w_words[0].rearrange("p n t -> p (n t)"), R, U32)
         list1 = load_list("list1", offs)
         load_plane(nc.sync, xt_plane, xt_scales)
-        load_plane(nc.sync, w_plane, w_scales)
         xt = load_words("xt", xt_words[0], T, U16)
+        load_plane(nc.sync, w_plane, w_scales)
         list2 = load_list("list2", offs2)
         xo = load_words("xo", xo_words[0].rearrange("p n t -> p (n t)"), Z, U32)
         load_plane(nc.sync, w2_plane, w2_scales)
-        w = load_words("w", w_words[0].rearrange("p n t -> p (n t)"), R, U32)
         load_plane(nc.sync, xo_plane, xo_scales)
         w2 = load_words("w2", w2_words[0], R, U16)
         wb = load_words("wb", wb_words[0], N, U16)
@@ -140,15 +140,13 @@ def tile_list_productentries_kernel(
         a_sum = first_stage("a", list1, xt, xt_plane, U16, FP4X4, w, w_plane, U32, FP8X4)
         b_sum = first_stage("b", list2, xo, xo_plane, U32, FP8X4, w2, w2_plane, U16, FP4X4)
 
-        gated = []
+        gated = tile("gated", [P, 2, HALF, PACK], F32, tag="xo_plane")
         for h in range(2):
-            prod = tile("gated%d" % h, [P, HALF, PACK], F32)
-            nc.vector.tensor_tensor(prod[:], a_sum[h][:].rearrange("p t j -> p j t"), gate_woven[h][:], MULT)
-            gated.append(prod)
+            nc.vector.tensor_tensor(gated[:, h], a_sum[h][:].rearrange("p t j -> p j t"), gate_woven[h][:], MULT)
         hid = []
         for h in range(2):
             larger = tile("hid%d" % h, [P, HALF, PACK], BF16)
-            nc.vector.tensor_tensor(larger[:], b_sum[h][:].rearrange("p t j -> p j t"), gated[h][:], MAX)
+            nc.vector.tensor_tensor(larger[:], b_sum[h][:].rearrange("p t j -> p j t"), gated[:, h], MAX)
             hid.append(larger)
 
         out_rows = out.rearrange("(c p) j -> p c j", p=P)

from contextlib import ExitStack

import concourse.mybir as mybir

F32 = mybir.dt.float32
BF16 = mybir.dt.bfloat16
I32 = mybir.dt.int32
U32 = mybir.dt.uint32
U16 = mybir.dt.uint16
U8 = mybir.dt.uint8
FP8 = mybir.dt.float8_e4m3fn
FP8X4 = mybir.dt.float8_e4m3fn_x4
FP4X4 = mybir.dt.float4_e2m1fn_x4
MULT = mybir.AluOpType.mult
MAX = mybir.AluOpType.max
COPY = mybir.ActivationFunctionType.Copy

P = 128
PACK = 4
T, J, R, Z, V, D, N = 1024, 256, 512, 1024, 1024, 512, 256
HALF = J // 2
FLOPS = 2 * 512 * R * J * 2 + 2 * R * N * J


def tile_list_productentries_kernel(
    tc, xt_words, xt_scales, xo_words, xo_scales, w_words, w_scales, w2_words, w2_scales,
    ca, cb, st, wb_words, wb_scales, offs, offs2, offs3, offs4, out,
):
    nc = tc.nc
    with ExitStack() as ctx:
        sb = ctx.enter_context(tc.tile_pool(name="sb", bufs=1))
        ps = ctx.enter_context(tc.psum_pool(name="ps", bufs=1))

        def tile(name, shape, dtype, tag=""):
            return sb.tile(shape, dtype, name=name, tag=tag, align_bytes=64)

        def load_list(name, src):
            lst = tile(name, [P, J // 16], U16)
            nc.sync.dma_start(lst[:], src)
            return lst

        def load_words(name, src, width, dtype):
            words = tile(name, [P, width], dtype)
            nc.sync.dma_start(words[:].bitcast(I32), src.bitcast(I32))
            return words

        def zero_plane(engine, name, width):
            plane = tile(name, [P, width], U8, tag=name)
            engine.memset(plane[:].bitcast(I32), 0)
            return plane

        def load_plane(queue, plane, src):
            for q in range(4):
                queue.dma_start(
                    plane[32 * q : 32 * q + 4, :].bitcast(I32), src[0, 4 * q : 4 * q + 4, :].bitcast(I32)
                )

        def load_table(name, rows, width):
            table = tile(name, [P, width], U8)
            nc.sync.dma_start(table[:], rows)
            return table

        ca_rows = ca.rearrange("(p t) v -> t p v", t=PACK)
        cb_rows = cb.rearrange("(p t) d -> t p d", t=PACK)
        step = tile("step", [P, PACK], F32)
        cb_tab = {}
        ca_tab = {}

        xt_plane = zero_plane(nc.vector, "xt_plane", T)
        w_plane = zero_plane(nc.vector, "w_plane", R)
        w2_plane = zero_plane(nc.vector, "w2_plane", R)
        xo_plane = zero_plane(nc.vector, "xo_plane", Z)
        wb_plane = zero_plane(nc.vector, "wb_plane", N)

        list4 = load_list("list4", offs4)
        for t in range(PACK):
            cb_tab[t] = load_table("cb_tab%d" % t, cb_rows[t], D)
        nc.sync.dma_start(step[:], st.rearrange("(p t) o -> p (t o)", t=PACK))
        list3 = load_list("list3", offs3)
        for t in range(PACK):
            ca_tab[t] = load_table("ca_tab%d" % t, ca_rows[t], V)
        w = load_words("w", w_words[0].rearrange("p n t -> p (n t)"), R, U32)
        list1 = load_list("list1", offs)
        load_plane(nc.sync, xt_plane, xt_scales)
        xt = load_words("xt", xt_words[0], T, U16)
        load_plane(nc.sync, w_plane, w_scales)
        list2 = load_list("list2", offs2)
        xo = load_words("xo", xo_words[0].rearrange("p n t -> p (n t)"), Z, U32)
        load_plane(nc.sync, w2_plane, w2_scales)
        load_plane(nc.sync, xo_plane, xo_scales)
        w2 = load_words("w2", w2_words[0], R, U16)
        wb = load_words("wb", wb_words[0], N, U16)
        load_plane(nc.sync, wb_plane, wb_scales)

        ca_pick = tile("ca_pick", [P, PACK, J], U8)
        cb_pick = tile("cb_pick", [P, PACK, J], U8)
        cb_step = tile("cb_step", [P, PACK, J], F32)
        gate = tile("gate", [P, PACK, J], F32)
        for t in range(PACK):
            nc.vector.tensor_copy(cb_pick[:, t, :], cb_tab[t][:].indirect(list4[:]))
            nc.scalar.activation(
                out=cb_step[:, t, :], in_=cb_pick[:, t, :].bitcast(FP8), func=COPY, scale=step[:, t : t + 1]
            )
        for t in range(PACK):
            nc.vector.tensor_copy(ca_pick[:, t, :], ca_tab[t][:].indirect(list3[:]))
        nc.vector.tensor_tensor(gate[:], ca_pick[:].bitcast(FP8), cb_step[:], MULT)

        gate_woven = []
        for h in range(2):
            woven = tile("gate_woven%d" % h, [P, HALF, PACK], F32)
            nc.scalar.copy(woven[:], gate[:, :, h * HALF : (h + 1) * HALF].rearrange("p t j -> p j t"))
            gate_woven.append(woven)

        def first_stage(name, lst, x, x_plane, x_dt, x_mx, wt, wt_plane, wt_dt, wt_mx):
            wt_dealt = tile(name + "_w_dealt", [P, PACK, P], wt_dt)
            nc.scalar.copy(wt_dealt[:], wt[:].rearrange("p (m t) -> p t m", t=PACK))
            ws_dealt = tile(name + "_ws_dealt", [P, PACK, P], U8)
            nc.vector.tensor_copy(ws_dealt[:], wt_plane[:].rearrange("p (m t) -> p t m", t=PACK))
            x_pick = tile(name + "_x_pick", [P, J], x_dt)
            nc.vector.tensor_copy(x_pick[:], x[:].indirect(lst[:]))
            xs_pick = tile(name + "_xs_pick", [P, J], U8)
            nc.vector.tensor_copy(xs_pick[:], x_plane[:].indirect(lst[:]))
            banks = []
            for h in range(2):
                bank = ps.tile([P, PACK, HALF], F32, name="%s_sum%d" % (name, h))
                cols = slice(h * HALF, (h + 1) * HALF)
                for t in range(PACK):
                    nc.tensor.matmul_mx(
                        out=bank[:, t, :],
                        lhsT=wt_dealt[:, t, :].bitcast(wt_mx),
                        lhsT_scale=ws_dealt[:, t, :],
                        rhs=x_pick[:, cols].bitcast(x_mx),
                        rhs_scale=xs_pick[:, cols],
                        start=True,
                        stop=True,
                    )
                banks.append(bank)
            return banks

        a_sum = first_stage("a", list1, xt, xt_plane, U16, FP4X4, w, w_plane, U32, FP8X4)
        b_sum = first_stage("b", list2, xo, xo_plane, U32, FP8X4, w2, w2_plane, U16, FP4X4)

        gated = tile("gated", [P, 2, HALF, PACK], F32, tag="xo_plane")
        for h in range(2):
            nc.vector.tensor_tensor(gated[:, h], a_sum[h][:].rearrange("p t j -> p j t"), gate_woven[h][:], MULT)
        hid = []
        for h in range(2):
            larger = tile("hid%d" % h, [P, HALF, PACK], BF16)
            nc.vector.tensor_tensor(larger[:], b_sum[h][:].rearrange("p t j -> p j t"), gated[:, h], MAX)
            hid.append(larger)

        out_rows = out.rearrange("(c p) j -> p c j", p=P)
        for h in range(2):
            codes = tile("hid_codes%d" % h, [P, HALF], U32)
            scales = tile("hid_scales%d" % h, [P, HALF], U8)
            nc.vector.quantize_mx(
                out=codes[:].bitcast(FP8X4), scales=scales[:], in_=hid[h][:].rearrange("p j t -> p (j t)")
            )
            result = tile("result%d" % h, [P, N // P, HALF], F32)
            for c in range(N // P):
                acc = ps.tile([P, HALF], F32, name="out_sum%d_%d" % (h, c))
                nc.tensor.matmul_mx(
                    out=acc[:],
                    lhsT=wb[:, c * P : (c + 1) * P].bitcast(FP4X4),
                    lhsT_scale=wb_plane[:, c * P : (c + 1) * P],
                    rhs=codes[:].bitcast(FP8X4),
                    rhs_scale=scales[:],
                    start=True,
                    stop=True,
                )
                if h == 1 and c == 1:
                    nc.vector.tensor_copy(result[:, c, :], acc[:])
                else:
                    nc.scalar.copy(result[:, c, :], acc[:])
            nc.sync.dma_start(out_rows[:, :, h * HALF : (h + 1) * HALF], result[:])
